import numpy as np
import ml_dtypes


def mxq(x, axis, fmt="e4m3"):
    dtype, down = {"e4m3": (ml_dtypes.float8_e4m3fn, 7), "e5m2": (ml_dtypes.float8_e5m2, 14)}[fmt]
    v = np.moveaxis(np.asarray(x, np.float32).astype(ml_dtypes.bfloat16).astype(np.float64), axis, -1)
    blocks = v.reshape(v.shape[:-1] + (-1, 32))
    amax = np.abs(blocks).max(-1, keepdims=True)
    byte = np.maximum(np.where(amax > 0, np.frexp(amax)[1] - 1 + 127, 0) - down, 1)
    scale = np.exp2(byte - 127.0)
    codes = (blocks / scale).astype(np.float32).astype(dtype).astype(np.float64)
    return np.moveaxis((codes * scale).reshape(v.shape), -1, axis)


WIDE = False


def mx_kscale(k):
    if not WIDE:
        return np.ones(k)
    levels = np.array([10, -10, 5, -5, 0])
    if k % 512:
        return np.exp2(np.random.permutation(np.resize(levels, k // 32))).repeat(32)
    a = np.empty((k // 512, 16))
    for p in range(k // 512):
        a[p, :8] = np.random.permutation(np.resize(levels, 8))
        for g in range(8):
            far = levels[np.abs(levels - a[p, g]) >= 10]
            a[p, g + 8] = far[np.random.randint(len(far))]
    return np.exp2(a.ravel()).repeat(32)


def f64(x):
    return np.asarray(x).astype(np.float64)


def striped(idx):
    return np.tile(np.asarray(idx).reshape(-1, 16).T, (8, 1)).astype(np.uint16)


def unstriped(offs):
    return offs[:16].T.reshape(-1).astype(np.int64)


E2M1 = np.array([0.0, 0.5, 1.0, 1.5, 2.0, 3.0, 4.0, 6.0, -0.0, -0.5, -1.0, -1.5, -2.0, -3.0, -4.0, -6.0])


def pack_weight(w, fmt):
    k, n = w.shape
    w = f64(np.asarray(w, np.float32).astype(ml_dtypes.bfloat16)).reshape(k // 32, 32, n)
    amax = np.abs(w).max(1)
    if fmt == "e4m3":
        byte = np.frexp(amax)[1] - 1 + 127 - 7
    else:
        mant, ex = np.frexp(amax / 6.0)
        byte = np.where(mant > 0.5, ex, ex - 1) + 127
    byte = np.clip(np.where(amax > 0, byte, 1), 1, 254)
    scaled = (w * np.exp2(127.0 - byte)[:, None, :]).reshape(k, n).astype(np.float32)
    by_word = np.ascontiguousarray(scaled.reshape(k // 512, 128, 4, n).transpose(0, 1, 3, 2))
    if fmt == "e4m3":
        words = by_word.astype(ml_dtypes.float8_e4m3fn).view(np.uint8)
    else:
        c = by_word.astype(ml_dtypes.float4_e2m1fn).view(np.uint8) & 0xF
        words = (c[..., 0::2] | (c[..., 1::2] << 4)).reshape(k // 512, 128, 2 * n)
    return np.ascontiguousarray(words), np.ascontiguousarray(byte.astype(np.uint8).reshape(k // 512, 16, n))


def unpack_weight(words, scales, fmt):
    g, _, n = scales.shape
    words = np.ascontiguousarray(words).reshape(g, 128, n, -1)
    if fmt == "e4m3":
        vals = words.view(ml_dtypes.float8_e4m3fn).astype(np.float64)
    else:
        nib = np.empty((g, 128, n, 4), np.uint8)
        nib[..., 0::2] = words & 0xF
        nib[..., 1::2] = words >> 4
        vals = E2M1[nib]
    vals = vals * np.repeat(np.exp2(scales.astype(np.float64) - 127.0), 8, axis=1)[..., None]
    return vals.transpose(0, 1, 3, 2).reshape(g * 512, n)


D, T, I, Q, E = 512, 2048, 512, 128, 512


def setup_inputs():
    n = np.random.standard_normal
    idx = np.random.permutation(T)[:I]
    fd = mx_kscale(D)
    fi = mx_kscale(I)
    ti = np.ones(T)
    ti[idx] = fi
    keysp = pack_weight(n((D, T)) / fd[:, None], "e4m3")
    return {
        "query": (n((D, Q)) * 0.25 / np.sqrt(D) * fd[:, None]).astype(np.float32),
        "keys_words": keysp[0],
        "keys_scales": keysp[1],
        "size": (np.random.uniform(0.5, 2.0, (1, I)) * fi).astype(np.float32),
        "vals": (n((E, T)) / ti).astype(np.float32),
        "gain": (np.random.uniform(0.5, 1.5, (1, E))).astype(np.float32),
        "gate": (np.random.uniform(0.3, 1.2, (Q, 1))).astype(np.float32),
        "res": (n((Q, E)) * 1.0).astype(np.float32),
        "offs": striped(idx),
    }


def reference(query, keys_words, keys_scales, size, vals, gain, gate, res, offs):
    idx = unstriped(offs)
    keysu = unpack_weight(keys_words, keys_scales, "e4m3")
    queryq = mxq(f64(query), 0, "e4m3")
    keysidxg = keysu[:, idx]
    a = queryq.T @ keysidxg
    p = np.exp(a - np.max(a, axis=1, keepdims=True))
    w = p * f64(size) / np.sum(p, axis=1, keepdims=True)
    wt = w.T
    vt = f64(vals)[:, idx].T
    wtq = mxq(wt, 0, "e4m3")
    vtq = mxq(vt, 0, "e4m3")
    o = wtq.T @ vtq
    nr = f64(gate) / np.sqrt(np.mean(np.square(o), axis=1, keepdims=True) + 0.0001)
    y = o * nr * f64(gain) + f64(res)
    return y

@@ -1,0 +1,201 @@
+from contextlib import ExitStack
+
+import concourse.mybir as mybir
+from concourse.masks import make_identity
+
+D, T, I, Q, E = 512, 2048, 512, 128, 512
+FLOPS = 2 * D * Q * I + 2 * I * Q * E
+
+F32 = mybir.dt.float32
+BF16 = mybir.dt.bfloat16
+I32 = mybir.dt.int32
+U32 = mybir.dt.uint32
+U16 = mybir.dt.uint16
+U8 = mybir.dt.uint8
+FP8X4 = mybir.dt.float8_e4m3fn_x4
+ACT = mybir.ActivationFunctionType
+ALU = mybir.AluOpType
+
+P = 128
+PACK = 4
+BLOCKS = E // P
+EPS = 0.0001
+
+
+def tile_attend_readscaled_kernel(tc, query, keys_words, keys_scales, size, vals, gain, gate, res, offs, out):
+    nc = tc.nc
+    with ExitStack() as ctx:
+        sb = ctx.enter_context(tc.tile_pool(name="sb", bufs=1))
+        ps = ctx.enter_context(tc.psum_pool(name="ps", bufs=1))
+
+        def dealt(ap):
+            return ap.rearrange("p (u b j) -> p b u j", u=2, j=16)
+
+        def slot_tile(slot, width, dtype):
+            return sb.tile([P, width], dtype, name="slot%d" % slot, tag="slot%d" % slot, align_bytes=64)
+
+        def rows_tile(which, width, dtype):
+            return sb.tile([P, width], dtype, name="rows%d" % which, tag="rows%d" % which, align_bytes=64)
+
+        def column_tile(width):
+            return sb.tile([P, width], F32, name="columns", tag="columns", bufs=2)
+
+        offsets = sb.tile([P, I // 16], U16, name="offsets")
+        nc.sync.dma_start(offsets[:], offs)
+        size4 = column_tile(PACK)
+        nc.scalar.dma_start(size4[:], size.rearrange("o (p t) -> p (o t)", t=PACK))
+        gate_col = column_tile(1)
+        nc.scalar.dma_start(gate_col[:], gate)
+        q_raw = slot_tile(1, PACK * Q, F32)
+        key_pool = slot_tile(2, T, U32)
+        nc.sync.dma_start(key_pool[:].bitcast(I32), keys_words[0].rearrange("p n t -> p (n t)").bitcast(I32))
+        scale_pool = sb.tile([P, T], U8, name="scale_pool")
+        nc.gpsimd.memset(scale_pool[:].bitcast(I32), 0)
+        for quad in range(4):
+            nc.scalar.dma_start(
+                scale_pool[32 * quad : 32 * quad + 4, :].bitcast(I32),
+                keys_scales[0, 4 * quad : 4 * quad + 4, :].bitcast(I32),
+            )
+        nc.sync.dma_start(q_raw[:], query.rearrange("(p t) q -> p (t q)", t=PACK))
+
+        def load_vals(c):
+            val_pool = slot_tile(c % 3, T, F32)
+            nc.sync.dma_start(val_pool[:], vals[c * P : (c + 1) * P, :])
+            return val_pool
+
+        val_pools = [load_vals(0)]
+        ident = sb.tile([P, P], F32, name="ident")
+        make_identity(nc, ident[:])
+
+        def spread(cols):
+            bank = ps.tile([P, PACK, P], F32, name="turn", tag="turn", bufs=3)
+            for t in range(PACK):
+                nc.tensor.transpose(bank[:, t, :], cols[:, t : t + 1].to_broadcast([P, P]), ident[:])
+            return bank
+
+        def turn(rows, name):
+            words = rows[:].bitcast(F32)
+            bank = ps.tile([P, 2, P], F32, name="turn", tag="turn", bufs=3)
+            for u in range(2):
+                nc.tensor.transpose(bank[:, u, :], words[:, u * P : (u + 1) * P], ident[:])
+            woven = sb.tile([P, P * PACK], BF16, name=name + "_woven", align_bytes=64)
+            nc.scalar.copy(
+                woven[:].bitcast(F32).rearrange("p (x u) -> p x u", u=2), bank[:].rearrange("p u x -> p x u")
+            )
+            return woven
+
+        def quantise(woven, codes, name):
+            scales = sb.tile([P, P], U8, name=name + "_scales", align_bytes=64)
+            nc.vector.quantize_mx(out=codes[:].bitcast(FP8X4), scales=scales[:], in_=woven[:])
+            return scales
+
+        key_scales = sb.tile([P, I], U8, name="key_scales", align_bytes=64)
+        nc.vector.tensor_copy(key_scales[:], scale_pool[:].indirect(offsets[:]))
+        key_codes = rows_tile(0, I, U32)
+        nc.vector.tensor_copy(key_codes[:], key_pool[:].indirect(offsets[:]))
+        q_woven = sb.tile([P, Q, PACK], BF16, name="q_woven", align_bytes=64)
+        nc.scalar.copy(q_woven[:], q_raw[:].rearrange("p (t q) -> p q t", t=PACK))
+        val_pools.append(load_vals(1))
+        val_pools.append(load_vals(2))
+        q_codes = sb.tile([P, Q], U32, name="q_codes", align_bytes=64)
+        q_scales = sb.tile([P, Q], U8, name="q_scales", align_bytes=64)
+        nc.vector.quantize_mx(
+            out=q_codes[:].bitcast(FP8X4), scales=q_scales[:], in_=q_woven[:].rearrange("p q t -> p (q t)")
+        )
+        scores = ps.tile([P, I], F32, name="scores")
+        nc.tensor.matmul_mx(
+            out=scores[:],
+            lhsT=q_codes[:].bitcast(FP8X4),
+            lhsT_scale=q_scales[:],
+            rhs=key_codes[:].bitcast(FP8X4),
+            rhs_scale=key_scales[:],
+            start=True,
+            stop=True,
+        )
+
+        size_bank = spread(size4)
+        size_rows = sb.tile([P, I], F32, name="size_rows")
+        nc.scalar.copy(
+            size_rows[:].rearrange("p (u b h t) -> p u b h t", u=2, h=4, t=PACK),
+            size_bank[:].rearrange("p t (b u h) -> p u b h t", u=2, h=4),
+        )
+        gain4 = column_tile(PACK)
+        nc.scalar.dma_start(gain4[:], gain.rearrange("o (p t) -> p (o t)", t=PACK))
+        gain_bank = spread(gain4)
+        gain_gate = sb.tile([P, E], F32, name="gain_gate")
+        nc.scalar.activation(
+            gain_gate[:].rearrange("p (n t) -> p n t", t=PACK),
+            gain_bank[:].rearrange("p t n -> p n t"),
+            ACT.Copy,
+            scale=gate_col[:],
+        )
+
+        neg_max = sb.tile([P, 1], F32, name="neg_max")
+        nc.vector.tensor_reduce(neg_max[:], scores[:], mybir.AxisListType.X, ALU.max, negate=True)
+        probs = sb.tile([P, I], F32, name="probs")
+        row_sum = sb.tile([P, 1], F32, name="row_sum")
+        nc.scalar.activation(
+            dealt(probs[:]),
+            scores[:].rearrange("p (b u j) -> p b u j", u=2, j=16),
+            ACT.Exp,
+            bias=neg_max[:],
+            accum_out=row_sum[:],
+        )
+        warm = sb.tile([P, 1], F32, name="warm")
+        nc.scalar.activation(warm[:], row_sum[:], ACT.Abs_reciprocal_sqrt)
+        inv_sum = sb.tile([P, 1], F32, name="inv_sum")
+        nc.vector.reciprocal(inv_sum[:], row_sum[:])
+        weights = rows_tile(1, I, BF16)
+        nc.vector.scalar_tensor_tensor(weights[:], probs[:], inv_sum[:], size_rows[:], ALU.mult, ALU.mult)
+        w_codes = sb.tile([P, P], U32, name="w_codes", align_bytes=64)
+        w_scales = quantise(turn(weights, "w"), w_codes, "w")
+
+        HALF = E // 2
+        reads = [ps.tile([P, HALF], F32, name="read%d" % h) for h in range(2)]
+
+        def pick(c):
+            picked = rows_tile(c % 2, I, BF16)
+            nc.vector.tensor_copy(dealt(picked[:]), val_pools[c][:].indirect(offsets[:]))
+            return turn(picked, "v%d" % c)
+
+        def multiply(c, woven, v_codes):
+            v_scales = quantise(woven, v_codes, "v%d" % c)
+            nc.tensor.matmul_mx(
+                out=reads[c // 2][:, (c % 2) * P : (c % 2 + 1) * P],
+                lhsT=w_codes[:].bitcast(FP8X4),
+                lhsT_scale=w_scales[:],
+                rhs=v_codes[:].bitcast(FP8X4),
+                rhs_scale=v_scales[:],
+                start=True,
+                stop=True,
+            )
+
+        squares = sb.tile([P, HALF], F32, name="squares")
+        sums = [sb.tile([P, 1], F32, name="sum%d" % h) for h in range(2)]
+        wovens = [pick(0)]
+        val_pools.append(load_vals(3))
+        for c in range(1, BLOCKS):
+            wovens.append(pick(c))
+            multiply(c - 1, wovens[c - 1], slot_tile(c % 3, P, U32))
+            if c == 1:
+                res_sb = slot_tile(1, E, F32)
+                nc.sync.dma_start(res_sb[:], res)
+            if c == 2:
+                nc.scalar.activation(squares[:], reads[0][:], ACT.Square, accum_out=sums[0][:])
+                head_eps = sb.tile([P, 1], F32, name="head_eps")
+                nc.scalar.activation(head_eps[:], sums[0][:], ACT.Copy, bias=EPS, scale=1.0 / E)
+        gained = [rows_tile(1, HALF, F32), sb.tile([P, HALF], F32, name="gained1")]
+        nc.vector.tensor_tensor(gained[0][:], reads[0][:], gain_gate[:, 0:HALF], ALU.mult)
+        last_codes = sb.tile([P, P], U32, name="last_codes", align_bytes=64)
+        multiply(BLOCKS - 1, wovens[BLOCKS - 1], last_codes)
+        nc.scalar.activation(squares[:], reads[1][:], ACT.Square, accum_out=sums[1][:])
+        nc.vector.tensor_tensor(gained[1][:], reads[1][:], gain_gate[:, HALF:E], ALU.mult)
+        inv_rms = sb.tile([P, 1], F32, name="inv_rms")
+        nc.scalar.activation(inv_rms[:], sums[1][:], ACT.Abs_reciprocal_sqrt, bias=head_eps[:], scale=1.0 / E)
+        result = sb.tile([P, E], F32, name="result")
+        for h, queue in enumerate((nc.sync, nc.scalar)):
+            cols = slice(h * E // 2, (h + 1) * E // 2)
+            nc.vector.scalar_tensor_tensor(
+                result[:, cols], gained[h][:], inv_rms[:], res_sb[:, cols], ALU.mult, ALU.add
+            )
+            queue.dma_start(out[:, cols], result[:, cols])

@@ -22,33 +22,21 @@ BLOCKS = E // P
 EPS = 0.0001
 
 
+HALF = E // 2
+SLOT = T * 4
+SPARE = 1024
+
+
 def tile_attend_readscaled_kernel(tc, query, keys_words, keys_scales, size, vals, gain, gate, res, offs, out):
     nc = tc.nc
     with ExitStack() as ctx:
         sb = ctx.enter_context(tc.tile_pool(name="sb", bufs=1))
+        slots = ctx.enter_context(tc.tile_pool(name="slots", bufs=1))
         ps = ctx.enter_context(tc.psum_pool(name="ps", bufs=1))
 
-        def dealt(ap):
-            return ap.rearrange("p (u b j) -> p b u j", u=2, j=16)
+        def after_pick(c, place, width, dtype, name):
+            return slots.tile([P, width], dtype, name=name, offset=c * SLOT + place * SPARE, align_bytes=64)
 
-        def slot_tile(slot, width, dtype):
-            return sb.tile([P, width], dtype, name="slot%d" % slot, tag="slot%d" % slot, align_bytes=64)
-
-        def rows_tile(which, width, dtype):
-            return sb.tile([P, width], dtype, name="rows%d" % which, tag="rows%d" % which, align_bytes=64)
-
-        def column_tile(width):
-            return sb.tile([P, width], F32, name="columns", tag="columns", bufs=2)
-
-        offsets = sb.tile([P, I // 16], U16, name="offsets")
-        nc.sync.dma_start(offsets[:], offs)
-        size4 = column_tile(PACK)
-        nc.scalar.dma_start(size4[:], size.rearrange("o (p t) -> p (o t)", t=PACK))
-        gate_col = column_tile(1)
-        nc.scalar.dma_start(gate_col[:], gate)
-        q_raw = slot_tile(1, PACK * Q, F32)
-        key_pool = slot_tile(2, T, U32)
-        nc.sync.dma_start(key_pool[:].bitcast(I32), keys_words[0].rearrange("p n t -> p (n t)").bitcast(I32))
         scale_pool = sb.tile([P, T], U8, name="scale_pool")
         nc.gpsimd.memset(scale_pool[:].bitcast(I32), 0)
         for quad in range(4):
@@ -56,14 +44,25 @@ def tile_attend_readscaled_kernel(tc, query, keys_words, keys_scales, size, vals
                 scale_pool[32 * quad : 32 * quad + 4, :].bitcast(I32),
                 keys_scales[0, 4 * quad : 4 * quad + 4, :].bitcast(I32),
             )
-        nc.sync.dma_start(q_raw[:], query.rearrange("(p t) q -> p (t q)", t=PACK))
+        offsets = sb.tile([P, I // 16], U16, name="offsets")
+        nc.sync.dma_start(offsets[:], offs)
+        key_pool = sb.tile([P, T], U32, name="key_pool")
+        nc.sync.dma_start(key_pool[:].bitcast(I32), keys_words[0].rearrange("p n t -> p (n t)").bitcast(I32))
+        q_raw = sb.tile([P, PACK, Q], F32, name="q_raw")
+        nc.sync.dma_start(q_raw[:], query.rearrange("(p t) q -> p t q", t=PACK))
+        size4 = sb.tile([P, PACK], F32, name="size4")
+        nc.sync.dma_start(size4[:], size.rearrange("o (p t) -> p (o t)", t=PACK))
+        val_pools = [after_pick(c, 0, T, F32, "val_pool%d" % c) for c in range(BLOCKS)]
+        nc.sync.dma_start(val_pools[0][:], vals[0:P, :])
+        gain4 = sb.tile([P, PACK], F32, name="gain4")
+        nc.sync.dma_start(gain4[:], gain.rearrange("o (p t) -> p (o t)", t=PACK))
+        gate_col = sb.tile([P, 1], F32, name="gate_col")
+        nc.sync.dma_start(gate_col[:], gate)
+        for c in range(1, BLOCKS):
+            nc.sync.dma_start(val_pools[c][:], vals[c * P : (c + 1) * P, :])
+        res_sb = sb.tile([P, E], F32, name="res_sb")
+        nc.sync.dma_start(res_sb[:], res)
 
-        def load_vals(c):
-            val_pool = slot_tile(c % 3, T, F32)
-            nc.sync.dma_start(val_pool[:], vals[c * P : (c + 1) * P, :])
-            return val_pool
-
-        val_pools = [load_vals(0)]
         ident = sb.tile([P, P], F32, name="ident")
         make_identity(nc, ident[:])
 
@@ -71,13 +70,13 @@ def tile_attend_readscaled_kernel(tc, query, keys_words, keys_scales, size, vals
             bank = ps.tile([P, PACK, P], F32, name="turn", tag="turn", bufs=3)
             for t in range(PACK):
                 nc.tensor.transpose(bank[:, t, :], cols[:, t : t + 1].to_broadcast([P, P]), ident[:])
-            return bank
+            return bank[:].rearrange("p t n -> p n t")
 
         def turn(rows, name):
             words = rows[:].bitcast(F32)
             bank = ps.tile([P, 2, P], F32, name="turn", tag="turn", bufs=3)
             for u in range(2):
-                nc.tensor.transpose(bank[:, u, :], words[:, u * P : (u + 1) * P], ident[:])
+                nc.tensor.transpose(bank[:, u, :], words[:, u : I // 2 : 2], ident[:])
             woven = sb.tile([P, P * PACK], BF16, name=name + "_woven", align_bytes=64)
             nc.scalar.copy(
                 woven[:].bitcast(F32).rearrange("p (x u) -> p x u", u=2), bank[:].rearrange("p u x -> p x u")
@@ -89,19 +88,19 @@ def tile_attend_readscaled_kernel(tc, query, keys_words, keys_scales, size, vals
             nc.vector.quantize_mx(out=codes[:].bitcast(FP8X4), scales=scales[:], in_=woven[:])
             return scales
 
+        def pick(c):
+            picked = sb.tile([P, I], BF16, name="picked%d" % c)
+            nc.vector.tensor_copy(picked[:], val_pools[c][:].indirect(offsets[:]))
+            return turn(picked, "v%d" % c)
+
+        key_codes = sb.tile([P, I], U32, name="key_codes", align_bytes=64)
+        nc.vector.tensor_copy(key_codes[:], key_pool[:].indirect(offsets[:]))
         key_scales = sb.tile([P, I], U8, name="key_scales", align_bytes=64)
         nc.vector.tensor_copy(key_scales[:], scale_pool[:].indirect(offsets[:]))
-        key_codes = rows_tile(0, I, U32)
-        nc.vector.tensor_copy(key_codes[:], key_pool[:].indirect(offsets[:]))
-        q_woven = sb.tile([P, Q, PACK], BF16, name="q_woven", align_bytes=64)
-        nc.scalar.copy(q_woven[:], q_raw[:].rearrange("p (t q) -> p q t", t=PACK))
-        val_pools.append(load_vals(1))
-        val_pools.append(load_vals(2))
+        q_woven = sb.tile([P, Q * PACK], BF16, name="q_woven", align_bytes=64)
+        nc.scalar.copy(q_woven[:].rearrange("p (q t) -> p q t", t=PACK), q_raw[:].rearrange("p t q -> p q t"))
         q_codes = sb.tile([P, Q], U32, name="q_codes", align_bytes=64)
-        q_scales = sb.tile([P, Q], U8, name="q_scales", align_bytes=64)
-        nc.vector.quantize_mx(
-            out=q_codes[:].bitcast(FP8X4), scales=q_scales[:], in_=q_woven[:].rearrange("p q t -> p (q t)")
-        )
+        q_scales = quantise(q_woven, q_codes, "q")
         scores = ps.tile([P, I], F32, name="scores")
         nc.tensor.matmul_mx(
             out=scores[:],
@@ -113,88 +112,78 @@ def tile_attend_readscaled_kernel(tc, query, keys_words, keys_scales, size, vals
             stop=True,
         )
 
-        size_bank = spread(size4)
         size_rows = sb.tile([P, I], F32, name="size_rows")
-        nc.scalar.copy(
-            size_rows[:].rearrange("p (u b h t) -> p u b h t", u=2, h=4, t=PACK),
-            size_bank[:].rearrange("p t (b u h) -> p u b h t", u=2, h=4),
-        )
-        gain4 = column_tile(PACK)
-        nc.scalar.dma_start(gain4[:], gain.rearrange("o (p t) -> p (o t)", t=PACK))
-        gain_bank = spread(gain4)
+        nc.scalar.copy(size_rows[:].rearrange("p (n t) -> p n t", t=PACK), spread(size4))
         gain_gate = sb.tile([P, E], F32, name="gain_gate")
         nc.scalar.activation(
-            gain_gate[:].rearrange("p (n t) -> p n t", t=PACK),
-            gain_bank[:].rearrange("p t n -> p n t"),
-            ACT.Copy,
-            scale=gate_col[:],
+            gain_gate[:].rearrange("p (n t) -> p n t", t=PACK), spread(gain4), ACT.Copy, scale=gate_col[:]
         )
 
-        neg_max = sb.tile([P, 1], F32, name="neg_max")
+        wovens = [pick(0)]
+        neg_max = after_pick(0, 0, 1, F32, "neg_max")
         nc.vector.tensor_reduce(neg_max[:], scores[:], mybir.AxisListType.X, ALU.max, negate=True)
         probs = sb.tile([P, I], F32, name="probs")
         row_sum = sb.tile([P, 1], F32, name="row_sum")
-        nc.scalar.activation(
-            dealt(probs[:]),
-            scores[:].rearrange("p (b u j) -> p b u j", u=2, j=16),
-            ACT.Exp,
-            bias=neg_max[:],
-            accum_out=row_sum[:],
-        )
+        nc.scalar.activation(probs[:], scores[:], ACT.Exp, bias=neg_max[:], accum_out=row_sum[:])
         warm = sb.tile([P, 1], F32, name="warm")
         nc.scalar.activation(warm[:], row_sum[:], ACT.Abs_reciprocal_sqrt)
-        inv_sum = sb.tile([P, 1], F32, name="inv_sum")
+
+        wovens.append(pick(1))
+        inv_sum = after_pick(1, 0, 1, F32, "inv_sum")
         nc.vector.reciprocal(inv_sum[:], row_sum[:])
-        weights = rows_tile(1, I, BF16)
+        weights = sb.tile([P, I], BF16, name="weights")
         nc.vector.scalar_tensor_tensor(weights[:], probs[:], inv_sum[:], size_rows[:], ALU.mult, ALU.mult)
-        w_codes = sb.tile([P, P], U32, name="w_codes", align_bytes=64)
-        w_scales = quantise(turn(weights, "w"), w_codes, "w")
+        w_woven = turn(weights, "w")
 
-        HALF = E // 2
-        reads = [ps.tile([P, HALF], F32, name="read%d" % h) for h in range(2)]
+        read_head = ps.tile([P, HALF], F32, name="read_head")
+        reads = [read_head[:, 0:P], read_head[:, P:HALF]]
+        reads.extend(ps.tile([P, P], F32, name="read%d" % c)[:] for c in (2, 3))
+        v_codes = [after_pick(c + 1, 1, P, U32, "v_codes%d" % c) for c in range(BLOCKS - 1)]
+        v_codes.append(sb.tile([P, P], U32, name="v_codes_last", align_bytes=64))
+        v_scales = [quantise(wovens[0], v_codes[0], "v0")]
 
-        def pick(c):
-            picked = rows_tile(c % 2, I, BF16)
-            nc.vector.tensor_copy(dealt(picked[:]), val_pools[c][:].indirect(offsets[:]))
-            return turn(picked, "v%d" % c)
+        wovens.append(pick(2))
+        w_codes = after_pick(2, 0, P, U32, "w_codes")
+        w_scales = quantise(w_woven, w_codes, "w")
 
-        def multiply(c, woven, v_codes):
-            v_scales = quantise(woven, v_codes, "v%d" % c)
+        def multiply(c):
             nc.tensor.matmul_mx(
-                out=reads[c // 2][:, (c % 2) * P : (c % 2 + 1) * P],
+                out=reads[c],
                 lhsT=w_codes[:].bitcast(FP8X4),
                 lhsT_scale=w_scales[:],
-                rhs=v_codes[:].bitcast(FP8X4),
-                rhs_scale=v_scales[:],
+                rhs=v_codes[c][:].bitcast(FP8X4),
+                rhs_scale=v_scales[c][:],
                 start=True,
                 stop=True,
             )
 
+        v_scales.append(quantise(wovens[1], v_codes[1], "v1"))
+        multiply(0)
+        multiply(1)
         squares = sb.tile([P, HALF], F32, name="squares")
-        sums = [sb.tile([P, 1], F32, name="sum%d" % h) for h in range(2)]
-        wovens = [pick(0)]
-        val_pools.append(load_vals(3))
-        for c in range(1, BLOCKS):
-            wovens.append(pick(c))
-            multiply(c - 1, wovens[c - 1], slot_tile(c % 3, P, U32))
-            if c == 1:
-                res_sb = slot_tile(1, E, F32)
-                nc.sync.dma_start(res_sb[:], res)
-            if c == 2:
-                nc.scalar.activation(squares[:], reads[0][:], ACT.Square, accum_out=sums[0][:])
-                head_eps = sb.tile([P, 1], F32, name="head_eps")
-                nc.scalar.activation(head_eps[:], sums[0][:], ACT.Copy, bias=EPS, scale=1.0 / E)
-        gained = [rows_tile(1, HALF, F32), sb.tile([P, HALF], F32, name="gained1")]
-        nc.vector.tensor_tensor(gained[0][:], reads[0][:], gain_gate[:, 0:HALF], ALU.mult)
-        last_codes = sb.tile([P, P], U32, name="last_codes", align_bytes=64)
-        multiply(BLOCKS - 1, wovens[BLOCKS - 1], last_codes)
-        nc.scalar.activation(squares[:], reads[1][:], ACT.Square, accum_out=sums[1][:])
-        nc.vector.tensor_tensor(gained[1][:], reads[1][:], gain_gate[:, HALF:E], ALU.mult)
+        sums = [sb.tile([P, 1], F32, name="sum%d" % h) for h in range(3)]
+        nc.scalar.activation(squares[:], read_head[:], ACT.Square, accum_out=sums[0][:])
+        mean01 = sb.tile([P, 1], F32, name="mean01")
+        nc.scalar.activation(mean01[:], sums[0][:], ACT.Copy, bias=EPS, scale=1.0 / E)
+
+        wovens.append(pick(3))
+        v_scales.append(quantise(wovens[2], v_codes[2], "v2"))
+        multiply(2)
+        gained = [after_pick(3, 0, HALF, F32, "gained0"), sb.tile([P, HALF], F32, name="gained1")]
+        nc.vector.tensor_tensor(gained[0][:], read_head[:], gain_gate[:, 0:HALF], ALU.mult)
+        v_scales.append(quantise(wovens[3], v_codes[3], "v3"))
+        nc.scalar.activation(squares[:, 0:P], reads[2], ACT.Square, accum_out=sums[1][:])
+        mean012 = sb.tile([P, 1], F32, name="mean012")
+        nc.scalar.activation(mean012[:], sums[1][:], ACT.Identity, bias=mean01[:], scale=1.0 / E)
+        nc.vector.tensor_tensor(gained[1][:, 0:P], reads[2], gain_gate[:, HALF : HALF + P], ALU.mult)
+        multiply(3)
+        nc.scalar.activation(squares[:, 0:P], reads[3], ACT.Square, accum_out=sums[2][:])
+        nc.vector.tensor_tensor(gained[1][:, P:HALF], reads[3], gain_gate[:, HALF + P : E], ALU.mult)
         inv_rms = sb.tile([P, 1], F32, name="inv_rms")
-        nc.scalar.activation(inv_rms[:], sums[1][:], ACT.Abs_reciprocal_sqrt, bias=head_eps[:], scale=1.0 / E)
+        nc.scalar.activation(inv_rms[:], sums[2][:], ACT.Abs_reciprocal_sqrt, bias=mean012[:], scale=1.0 / E)
         result = sb.tile([P, E], F32, name="result")
         for h, queue in enumerate((nc.sync, nc.scalar)):
-            cols = slice(h * E // 2, (h + 1) * E // 2)
+            cols = slice(h * HALF, (h + 1) * HALF)
             nc.vector.scalar_tensor_tensor(
                 result[:, cols], gained[h][:], inv_rms[:], res_sb[:, cols], ALU.mult, ALU.add
             )

@@ -37,47 +37,57 @@ def tile_attend_readscaled_kernel(tc, query, keys_words, keys_scales, size, vals
         def after_pick(c, place, width, dtype, name):
             return slots.tile([P, width], dtype, name=name, offset=c * SLOT + place * SPARE, align_bytes=64)
 
+        ident = sb.tile([P, P], F32, name="ident")
+        make_identity(nc, ident[:])
+
         scale_pool = sb.tile([P, T], U8, name="scale_pool")
         nc.gpsimd.memset(scale_pool[:].bitcast(I32), 0)
-        for quad in range(4):
-            nc.scalar.dma_start(
-                scale_pool[32 * quad : 32 * quad + 4, :].bitcast(I32),
+
+        scale_rows = sb.tile([P, T], U8, name="scale_rows")
+
+        def load_scales(queue, quad):
+            queue.dma_start(
+                scale_rows[32 * quad : 32 * quad + 4, :].bitcast(I32),
                 keys_scales[0, 4 * quad : 4 * quad + 4, :].bitcast(I32),
             )
-        offsets = sb.tile([P, I // 16], U16, name="offsets")
-        nc.sync.dma_start(offsets[:], offs)
-        key_pool = sb.tile([P, T], U32, name="key_pool")
-        nc.sync.dma_start(key_pool[:].bitcast(I32), keys_words[0].rearrange("p n t -> p (n t)").bitcast(I32))
+
         q_raw = sb.tile([P, PACK, Q], F32, name="q_raw")
         nc.sync.dma_start(q_raw[:], query.rearrange("(p t) q -> p t q", t=PACK))
+        offsets = sb.tile([P, I // 16], U16, name="offsets")
+        nc.sync.dma_start(offsets[:], offs)
+        for quad, queue in enumerate((nc.scalar, nc.scalar, nc.sync, nc.sync)):
+            load_scales(queue, quad)
         size4 = sb.tile([P, PACK], F32, name="size4")
-        nc.sync.dma_start(size4[:], size.rearrange("o (p t) -> p (o t)", t=PACK))
-        val_pools = [after_pick(c, 0, T, F32, "val_pool%d" % c) for c in range(BLOCKS)]
-        nc.sync.dma_start(val_pools[0][:], vals[0:P, :])
+        nc.scalar.dma_start(size4[:], size.rearrange("o (p t) -> p (o t)", t=PACK))
+        key_pool = sb.tile([P, T], U32, name="key_pool")
+        nc.sync.dma_start(key_pool[:].bitcast(I32), keys_words[0].rearrange("p n t -> p (n t)").bitcast(I32))
         gain4 = sb.tile([P, PACK], F32, name="gain4")
         nc.sync.dma_start(gain4[:], gain.rearrange("o (p t) -> p (o t)", t=PACK))
         gate_col = sb.tile([P, 1], F32, name="gate_col")
         nc.sync.dma_start(gate_col[:], gate)
-        for c in range(1, BLOCKS):
+        val_pools = [after_pick(c, 0, T, F32, "val_pool%d" % c) for c in range(BLOCKS)]
+        for c in range(BLOCKS):
             nc.sync.dma_start(val_pools[c][:], vals[c * P : (c + 1) * P, :])
         res_sb = sb.tile([P, E], F32, name="res_sb")
         nc.sync.dma_start(res_sb[:], res)
 
-        ident = sb.tile([P, P], F32, name="ident")
-        make_identity(nc, ident[:])
-
-        def spread(cols):
-            bank = ps.tile([P, PACK, P], F32, name="turn", tag="turn", bufs=3)
+        def spread(cols, tag):
+            bank = ps.tile([P, PACK, P], F32, name=tag, tag=tag)
             for t in range(PACK):
                 nc.tensor.transpose(bank[:, t, :], cols[:, t : t + 1].to_broadcast([P, P]), ident[:])
             return bank[:].rearrange("p t n -> p n t")
 
-        def turn(rows, name):
+        def woven_tile(name):
+            return sb.tile([P, P * PACK], BF16, name=name + "_woven", tag=name + "_woven", align_bytes=64)
+
+        def before_pick(c, width, dtype):
+            return sb.tile([P, width], dtype, name="picked%d" % c, tag="picked%d" % c, align_bytes=64)
+
+        def turn(rows, woven, tag="turn", bufs=3):
             words = rows[:].bitcast(F32)
-            bank = ps.tile([P, 2, P], F32, name="turn", tag="turn", bufs=3)
+            bank = ps.tile([P, 2, P], F32, name=tag, tag=tag, bufs=bufs)
             for u in range(2):
                 nc.tensor.transpose(bank[:, u, :], words[:, u : I // 2 : 2], ident[:])
-            woven = sb.tile([P, P * PACK], BF16, name=name + "_woven", align_bytes=64)
             nc.scalar.copy(
                 woven[:].bitcast(F32).rearrange("p (x u) -> p x u", u=2), bank[:].rearrange("p u x -> p x u")
             )
@@ -88,20 +98,26 @@ def tile_attend_readscaled_kernel(tc, query, keys_words, keys_scales, size, vals
             nc.vector.quantize_mx(out=codes[:].bitcast(FP8X4), scales=scales[:], in_=woven[:])
             return scales
 
-        def pick(c):
-            picked = sb.tile([P, I], BF16, name="picked%d" % c)
+        def pick(c, **bank):
+            picked = before_pick(c, I, BF16)
             nc.vector.tensor_copy(picked[:], val_pools[c][:].indirect(offsets[:]))
-            return turn(picked, "v%d" % c)
+            return turn(picked, woven_tile("v%d" % c), **bank)
 
-        key_codes = sb.tile([P, I], U32, name="key_codes", align_bytes=64)
-        nc.vector.tensor_copy(key_codes[:], key_pool[:].indirect(offsets[:]))
+        for quad in range(4):
+            live = slice(32 * quad, 32 * quad + 4)
+            nc.vector.tensor_copy(scale_pool[live, :].bitcast(I32), scale_rows[live, :].bitcast(I32))
         key_scales = sb.tile([P, I], U8, name="key_scales", align_bytes=64)
         nc.vector.tensor_copy(key_scales[:], scale_pool[:].indirect(offsets[:]))
         q_woven = sb.tile([P, Q * PACK], BF16, name="q_woven", align_bytes=64)
         nc.scalar.copy(q_woven[:].rearrange("p (q t) -> p q t", t=PACK), q_raw[:].rearrange("p t q -> p q t"))
         q_codes = sb.tile([P, Q], U32, name="q_codes", align_bytes=64)
         q_scales = quantise(q_woven, q_codes, "q")
-        scores = ps.tile([P, I], F32, name="scores")
+        size_rows = sb.tile([P, I], F32, name="size_rows")
+        nc.scalar.copy(size_rows[:].rearrange("p (n t) -> p n t", t=PACK), spread(size4, "scores"))
+
+        key_codes = before_pick(0, I, U32)
+        nc.vector.tensor_copy(key_codes[:], key_pool[:].indirect(offsets[:]))
+        scores = ps.tile([P, I], F32, name="scores", tag="scores")
         nc.tensor.matmul_mx(
             out=scores[:],
             lhsT=q_codes[:].bitcast(FP8X4),
@@ -112,39 +128,35 @@ def tile_attend_readscaled_kernel(tc, query, keys_words, keys_scales, size, vals
             stop=True,
         )
 
-        size_rows = sb.tile([P, I], F32, name="size_rows")
-        nc.scalar.copy(size_rows[:].rearrange("p (n t) -> p n t", t=PACK), spread(size4))
         gain_gate = sb.tile([P, E], F32, name="gain_gate")
         nc.scalar.activation(
-            gain_gate[:].rearrange("p (n t) -> p n t", t=PACK), spread(gain4), ACT.Copy, scale=gate_col[:]
+            gain_gate[:].rearrange("p (n t) -> p n t", t=PACK), spread(gain4, "first_turn"), ACT.Copy, scale=gate_col[:]
         )
 
-        wovens = [pick(0)]
-        neg_max = after_pick(0, 0, 1, F32, "neg_max")
+        neg_max = sb.tile([P, 1], F32, name="neg_max")
         nc.vector.tensor_reduce(neg_max[:], scores[:], mybir.AxisListType.X, ALU.max, negate=True)
-        probs = sb.tile([P, I], F32, name="probs")
-        row_sum = sb.tile([P, 1], F32, name="row_sum")
+        probs = before_pick(2, I, F32)
+        row_sum = sb.tile([P, 1], F32, name="row_sum", tag="v0_woven", align_bytes=64)
         nc.scalar.activation(probs[:], scores[:], ACT.Exp, bias=neg_max[:], accum_out=row_sum[:])
-        warm = sb.tile([P, 1], F32, name="warm")
-        nc.scalar.activation(warm[:], row_sum[:], ACT.Abs_reciprocal_sqrt)
+        inv_sum = sb.tile([P, 1], F32, name="inv_sum")
+        nc.scalar.activation(inv_sum[:], row_sum[:], ACT.Abs_reciprocal_sqrt, scale=row_sum[:])
 
-        wovens.append(pick(1))
-        inv_sum = after_pick(1, 0, 1, F32, "inv_sum")
-        nc.vector.reciprocal(inv_sum[:], row_sum[:])
-        weights = sb.tile([P, I], BF16, name="weights")
+        wovens = [pick(0, tag="first_turn", bufs=1), pick(1)]
+        weights = after_pick(1, 0, I, BF16, "weights")
         nc.vector.scalar_tensor_tensor(weights[:], probs[:], inv_sum[:], size_rows[:], ALU.mult, ALU.mult)
-        w_woven = turn(weights, "w")
+        w_woven = turn(weights, before_pick(3, P * PACK, BF16))
+
+        v_codes = [after_pick(slot, 1 + c, P, U32, "v_codes%d" % c) for c, slot in enumerate((2, 2, 3))]
+        v_codes.append(sb.tile([P, P], U32, name="v_codes_last", align_bytes=64))
+
+        wovens.append(pick(2))
+        v_scales = [quantise(wovens[c], v_codes[c], "v%d" % c) for c in range(2)]
+        w_codes = after_pick(2, 0, P, U32, "w_codes")
+        w_scales = quantise(w_woven, w_codes, "w")
 
         read_head = ps.tile([P, HALF], F32, name="read_head")
         reads = [read_head[:, 0:P], read_head[:, P:HALF]]
         reads.extend(ps.tile([P, P], F32, name="read%d" % c)[:] for c in (2, 3))
-        v_codes = [after_pick(c + 1, 1, P, U32, "v_codes%d" % c) for c in range(BLOCKS - 1)]
-        v_codes.append(sb.tile([P, P], U32, name="v_codes_last", align_bytes=64))
-        v_scales = [quantise(wovens[0], v_codes[0], "v0")]
-
-        wovens.append(pick(2))
-        w_codes = after_pick(2, 0, P, U32, "w_codes")
-        w_scales = quantise(w_woven, w_codes, "w")
 
         def multiply(c):
             nc.tensor.matmul_mx(
@@ -157,7 +169,6 @@ def tile_attend_readscaled_kernel(tc, query, keys_words, keys_scales, size, vals
                 stop=True,
             )
 
-        v_scales.append(quantise(wovens[1], v_codes[1], "v1"))
         multiply(0)
         multiply(1)
         squares = sb.tile([P, HALF], F32, name="squares")

@@ -23,6 +23,7 @@ EPS = 0.0001
 
 
 HALF = E // 2
+EARLY = E - P
 SLOT = T * 4
 SPARE = 1024
 
@@ -89,7 +90,7 @@ def tile_attend_readscaled_kernel(tc, query, keys_words, keys_scales, size, vals
             for u in range(2):
                 nc.tensor.transpose(bank[:, u, :], words[:, u : I // 2 : 2], ident[:])
             nc.scalar.copy(
-                woven[:].bitcast(F32).rearrange("p (x u) -> p x u", u=2), bank[:].rearrange("p u x -> p x u")
+                woven.bitcast(F32).rearrange("p (x u) -> p x u", u=2), bank[:].rearrange("p u x -> p x u")
             )
             return woven
 
@@ -98,10 +99,10 @@ def tile_attend_readscaled_kernel(tc, query, keys_words, keys_scales, size, vals
             nc.vector.quantize_mx(out=codes[:].bitcast(FP8X4), scales=scales[:], in_=woven[:])
             return scales
 
-        def pick(c, **bank):
+        def pick(c, woven, **bank):
             picked = before_pick(c, I, BF16)
             nc.vector.tensor_copy(picked[:], val_pools[c][:].indirect(offsets[:]))
-            return turn(picked, woven_tile("v%d" % c), **bank)
+            return turn(picked, woven, **bank)
 
         for quad in range(4):
             live = slice(32 * quad, 32 * quad + 4)
@@ -136,66 +137,60 @@ def tile_attend_readscaled_kernel(tc, query, keys_words, keys_scales, size, vals
         neg_max = sb.tile([P, 1], F32, name="neg_max")
         nc.vector.tensor_reduce(neg_max[:], scores[:], mybir.AxisListType.X, ALU.max, negate=True)
         probs = before_pick(2, I, F32)
-        row_sum = sb.tile([P, 1], F32, name="row_sum", tag="v0_woven", align_bytes=64)
+        row_sum = sb.tile([P, 1], F32, name="row_sum", tag="early_woven", align_bytes=64)
         nc.scalar.activation(probs[:], scores[:], ACT.Exp, bias=neg_max[:], accum_out=row_sum[:])
         inv_sum = sb.tile([P, 1], F32, name="inv_sum")
         nc.scalar.activation(inv_sum[:], row_sum[:], ACT.Abs_reciprocal_sqrt, scale=row_sum[:])
 
-        wovens = [pick(0, tag="first_turn", bufs=1), pick(1)]
+        early_woven = sb.tile([P, BLOCKS * I], BF16, name="early_woven", tag="early_woven", align_bytes=64)
+        pick(0, early_woven[:, 0:I], tag="first_turn", bufs=1)
+        pick(1, early_woven[:, I : 2 * I])
         weights = after_pick(1, 0, I, BF16, "weights")
         nc.vector.scalar_tensor_tensor(weights[:], probs[:], inv_sum[:], size_rows[:], ALU.mult, ALU.mult)
-        w_woven = turn(weights, before_pick(3, P * PACK, BF16))
+        turn(weights, early_woven[:, 3 * I : 4 * I])
+        pick(2, early_woven[:, 2 * I : 3 * I])
+        last_woven = woven_tile("last")
+        pick(3, last_woven[:])
 
-        v_codes = [after_pick(slot, 1 + c, P, U32, "v_codes%d" % c) for c, slot in enumerate((2, 2, 3))]
-        v_codes.append(sb.tile([P, P], U32, name="v_codes_last", align_bytes=64))
+        early_codes = after_pick(3, 1, BLOCKS * P, U32, "early_codes")
+        early_scales = sb.tile([P, BLOCKS * P], U8, name="early_scales", align_bytes=64)
+        nc.vector.quantize_mx(out=early_codes[:].bitcast(FP8X4), scales=early_scales[:], in_=early_woven[:])
+        last_codes = sb.tile([P, P], U32, name="last_codes", align_bytes=64)
+        last_scales = quantise(last_woven, last_codes, "last")
 
-        wovens.append(pick(2))
-        v_scales = [quantise(wovens[c], v_codes[c], "v%d" % c) for c in range(2)]
-        w_codes = after_pick(2, 0, P, U32, "w_codes")
-        w_scales = quantise(w_woven, w_codes, "w")
-
-        read_head = ps.tile([P, HALF], F32, name="read_head")
-        reads = [read_head[:, 0:P], read_head[:, P:HALF]]
-        reads.extend(ps.tile([P, P], F32, name="read%d" % c)[:] for c in (2, 3))
-
-        def multiply(c):
+        def multiply(read, codes, scales):
             nc.tensor.matmul_mx(
-                out=reads[c],
-                lhsT=w_codes[:].bitcast(FP8X4),
-                lhsT_scale=w_scales[:],
-                rhs=v_codes[c][:].bitcast(FP8X4),
-                rhs_scale=v_scales[c][:],
+                out=read,
+                lhsT=early_codes[:, EARLY:E].bitcast(FP8X4),
+                lhsT_scale=early_scales[:, EARLY:E],
+                rhs=codes.bitcast(FP8X4),
+                rhs_scale=scales,
                 start=True,
                 stop=True,
             )
 
-        multiply(0)
-        multiply(1)
-        squares = sb.tile([P, HALF], F32, name="squares")
-        sums = [sb.tile([P, 1], F32, name="sum%d" % h) for h in range(3)]
-        nc.scalar.activation(squares[:], read_head[:], ACT.Square, accum_out=sums[0][:])
-        mean01 = sb.tile([P, 1], F32, name="mean01")
-        nc.scalar.activation(mean01[:], sums[0][:], ACT.Copy, bias=EPS, scale=1.0 / E)
+        early_read = ps.tile([P, EARLY], F32, name="early_read")
+        for cols in (slice(0, HALF), slice(HALF, EARLY)):
+            multiply(early_read[:, cols], early_codes[:, cols], early_scales[:, cols])
+        last_read = ps.tile([P, P], F32, name="last_read")
+        multiply(last_read[:], last_codes[:], last_scales[:])
 
-        wovens.append(pick(3))
-        v_scales.append(quantise(wovens[2], v_codes[2], "v2"))
-        multiply(2)
-        gained = [after_pick(3, 0, HALF, F32, "gained0"), sb.tile([P, HALF], F32, name="gained1")]
-        nc.vector.tensor_tensor(gained[0][:], read_head[:], gain_gate[:, 0:HALF], ALU.mult)
-        v_scales.append(quantise(wovens[3], v_codes[3], "v3"))
-        nc.scalar.activation(squares[:, 0:P], reads[2], ACT.Square, accum_out=sums[1][:])
-        mean012 = sb.tile([P, 1], F32, name="mean012")
-        nc.scalar.activation(mean012[:], sums[1][:], ACT.Identity, bias=mean01[:], scale=1.0 / E)
-        nc.vector.tensor_tensor(gained[1][:, 0:P], reads[2], gain_gate[:, HALF : HALF + P], ALU.mult)
-        multiply(3)
-        nc.scalar.activation(squares[:, 0:P], reads[3], ACT.Square, accum_out=sums[2][:])
-        nc.vector.tensor_tensor(gained[1][:, P:HALF], reads[3], gain_gate[:, HALF + P : E], ALU.mult)
+        squares = sb.tile([P, E], F32, name="squares")
+        gained = sb.tile([P, E], F32, name="gained")
+        early_sum = sb.tile([P, 1], F32, name="early_sum")
+        nc.scalar.activation(squares[:, 0:EARLY], early_read[:], ACT.Square, accum_out=early_sum[:])
+        nc.vector.tensor_tensor(gained[:, 0:EARLY], early_read[:], gain_gate[:, 0:EARLY], ALU.mult)
+        early_mean = sb.tile([P, 1], F32, name="early_mean")
+        nc.scalar.activation(early_mean[:], early_sum[:], ACT.Copy, bias=EPS, scale=1.0 / E)
+        last_sum = sb.tile([P, 1], F32, name="last_sum")
+        nc.scalar.activation(squares[:, EARLY:E], last_read[:], ACT.Square, accum_out=last_sum[:])
+        nc.vector.tensor_tensor(gained[:, EARLY:E], last_read[:], gain_gate[:, EARLY:E], ALU.mult)
         inv_rms = sb.tile([P, 1], F32, name="inv_rms")
-        nc.scalar.activation(inv_rms[:], sums[2][:], ACT.Abs_reciprocal_sqrt, bias=mean012[:], scale=1.0 / E)
+        nc.scalar.activation(inv_rms[:], last_sum[:], ACT.Abs_reciprocal_sqrt, bias=early_mean[:], scale=1.0 / E)
         result = sb.tile([P, E], F32, name="result")
         for h, queue in enumerate((nc.sync, nc.scalar)):
             cols = slice(h * HALF, (h + 1) * HALF)
             nc.vector.scalar_tensor_tensor(
-                result[:, cols], gained[h][:], inv_rms[:], res_sb[:, cols], ALU.mult, ALU.add
+                result[:, cols], gained[:, cols], inv_rms[:], res_sb[:, cols], ALU.mult, ALU.add
             )
             queue.dma_start(out[:, cols], result[:, cols])

@@ -58,16 +58,17 @@ def tile_attend_readscaled_kernel(tc, query, keys_words, keys_scales, size, vals
         nc.sync.dma_start(offsets[:], offs)
         for quad, queue in enumerate((nc.scalar, nc.scalar, nc.sync, nc.sync)):
             load_scales(queue, quad)
-        size4 = sb.tile([P, PACK], F32, name="size4")
-        nc.scalar.dma_start(size4[:], size.rearrange("o (p t) -> p (o t)", t=PACK))
         key_pool = sb.tile([P, T], U32, name="key_pool")
         nc.sync.dma_start(key_pool[:].bitcast(I32), keys_words[0].rearrange("p n t -> p (n t)").bitcast(I32))
+        val_pools = [after_pick(c, 0, T, F32, "val_pool%d" % c) for c in range(BLOCKS)]
+        nc.sync.dma_start(val_pools[0][:], vals[0:P, :])
+        size4 = sb.tile([P, PACK], F32, name="size4")
+        nc.sync.dma_start(size4[:], size.rearrange("o (p t) -> p (o t)", t=PACK))
         gain4 = sb.tile([P, PACK], F32, name="gain4")
         nc.sync.dma_start(gain4[:], gain.rearrange("o (p t) -> p (o t)", t=PACK))
         gate_col = sb.tile([P, 1], F32, name="gate_col")
         nc.sync.dma_start(gate_col[:], gate)
-        val_pools = [after_pick(c, 0, T, F32, "val_pool%d" % c) for c in range(BLOCKS)]
-        for c in range(BLOCKS):
+        for c in range(1, BLOCKS):
             nc.sync.dma_start(val_pools[c][:], vals[c * P : (c + 1) * P, :])
         res_sb = sb.tile([P, E], F32, name="res_sb")
         nc.sync.dma_start(res_sb[:], res)
@@ -113,9 +114,6 @@ def tile_attend_readscaled_kernel(tc, query, keys_words, keys_scales, size, vals
         nc.scalar.copy(q_woven[:].rearrange("p (q t) -> p q t", t=PACK), q_raw[:].rearrange("p t q -> p q t"))
         q_codes = sb.tile([P, Q], U32, name="q_codes", align_bytes=64)
         q_scales = quantise(q_woven, q_codes, "q")
-        size_rows = sb.tile([P, I], F32, name="size_rows")
-        nc.scalar.copy(size_rows[:].rearrange("p (n t) -> p n t", t=PACK), spread(size4, "scores"))
-
         key_codes = before_pick(0, I, U32)
         nc.vector.tensor_copy(key_codes[:], key_pool[:].indirect(offsets[:]))
         scores = ps.tile([P, I], F32, name="scores", tag="scores")
@@ -129,10 +127,8 @@ def tile_attend_readscaled_kernel(tc, query, keys_words, keys_scales, size, vals
             stop=True,
         )
 
-        gain_gate = sb.tile([P, E], F32, name="gain_gate")
-        nc.scalar.activation(
-            gain_gate[:].rearrange("p (n t) -> p n t", t=PACK), spread(gain4, "first_turn"), ACT.Copy, scale=gate_col[:]
-        )
+        size_rows = sb.tile([P, I], F32, name="size_rows")
+        nc.scalar.copy(size_rows[:].rearrange("p (n t) -> p n t", t=PACK), spread(size4, "first_turn"))
 
         neg_max = sb.tile([P, 1], F32, name="neg_max")
         nc.vector.tensor_reduce(neg_max[:], scores[:], mybir.AxisListType.X, ALU.max, negate=True)
@@ -142,13 +138,18 @@ def tile_attend_readscaled_kernel(tc, query, keys_words, keys_scales, size, vals
         inv_sum = sb.tile([P, 1], F32, name="inv_sum")
         nc.scalar.activation(inv_sum[:], row_sum[:], ACT.Abs_reciprocal_sqrt, scale=row_sum[:])
 
+        gain_gate = sb.tile([P, E], F32, name="gain_gate")
+        nc.scalar.activation(
+            gain_gate[:].rearrange("p (n t) -> p n t", t=PACK), spread(gain4, "scores"), ACT.Copy, scale=gate_col[:]
+        )
+
         early_woven = sb.tile([P, BLOCKS * I], BF16, name="early_woven", tag="early_woven", align_bytes=64)
         pick(0, early_woven[:, 0:I], tag="first_turn", bufs=1)
         pick(1, early_woven[:, I : 2 * I])
         weights = after_pick(1, 0, I, BF16, "weights")
         nc.vector.scalar_tensor_tensor(weights[:], probs[:], inv_sum[:], size_rows[:], ALU.mult, ALU.mult)
         turn(weights, early_woven[:, 3 * I : 4 * I])
-        pick(2, early_woven[:, 2 * I : 3 * I])
+        pick(2, early_woven[:, 2 * I : 3 * I], tag="scores", bufs=1)
         last_woven = woven_tile("last")
         pick(3, last_woven[:])
 

from contextlib import ExitStack

import concourse.mybir as mybir
from concourse.masks import make_identity

D, T, I, Q, E = 512, 2048, 512, 128, 512
FLOPS = 2 * D * Q * I + 2 * I * Q * E

F32 = mybir.dt.float32
BF16 = mybir.dt.bfloat16
I32 = mybir.dt.int32
U32 = mybir.dt.uint32
U16 = mybir.dt.uint16
U8 = mybir.dt.uint8
FP8X4 = mybir.dt.float8_e4m3fn_x4
ACT = mybir.ActivationFunctionType
ALU = mybir.AluOpType

P = 128
PACK = 4
BLOCKS = E // P
EPS = 0.0001


HALF = E // 2
EARLY = E - P
SLOT = T * 4
SPARE = 1024


def tile_attend_readscaled_kernel(tc, query, keys_words, keys_scales, size, vals, gain, gate, res, offs, out):
    nc = tc.nc
    with ExitStack() as ctx:
        sb = ctx.enter_context(tc.tile_pool(name="sb", bufs=1))
        slots = ctx.enter_context(tc.tile_pool(name="slots", bufs=1))
        ps = ctx.enter_context(tc.psum_pool(name="ps", bufs=1))

        def after_pick(c, place, width, dtype, name):
            return slots.tile([P, width], dtype, name=name, offset=c * SLOT + place * SPARE, align_bytes=64)

        ident = sb.tile([P, P], F32, name="ident")
        make_identity(nc, ident[:])

        scale_pool = sb.tile([P, T], U8, name="scale_pool")
        nc.gpsimd.memset(scale_pool[:].bitcast(I32), 0)

        scale_rows = sb.tile([P, T], U8, name="scale_rows")

        def load_scales(queue, quad):
            queue.dma_start(
                scale_rows[32 * quad : 32 * quad + 4, :].bitcast(I32),
                keys_scales[0, 4 * quad : 4 * quad + 4, :].bitcast(I32),
            )

        q_raw = sb.tile([P, PACK, Q], F32, name="q_raw")
        nc.sync.dma_start(q_raw[:], query.rearrange("(p t) q -> p t q", t=PACK))
        offsets = sb.tile([P, I // 16], U16, name="offsets")
        nc.sync.dma_start(offsets[:], offs)
        for quad, queue in enumerate((nc.scalar, nc.scalar, nc.sync, nc.sync)):
            load_scales(queue, quad)
        key_pool = sb.tile([P, T], U32, name="key_pool")
        nc.sync.dma_start(key_pool[:].bitcast(I32), keys_words[0].rearrange("p n t -> p (n t)").bitcast(I32))
        val_pools = [after_pick(c, 0, T, F32, "val_pool%d" % c) for c in range(BLOCKS)]
        nc.sync.dma_start(val_pools[0][:], vals[0:P, :])
        size4 = sb.tile([P, PACK], F32, name="size4")
        nc.sync.dma_start(size4[:], size.rearrange("o (p t) -> p (o t)", t=PACK))
        gain4 = sb.tile([P, PACK], F32, name="gain4")
        nc.sync.dma_start(gain4[:], gain.rearrange("o (p t) -> p (o t)", t=PACK))
        gate_col = sb.tile([P, 1], F32, name="gate_col")
        nc.sync.dma_start(gate_col[:], gate)
        for c in range(1, BLOCKS):
            nc.sync.dma_start(val_pools[c][:], vals[c * P : (c + 1) * P, :])
        res_sb = sb.tile([P, E], F32, name="res_sb")
        nc.sync.dma_start(res_sb[:], res)

        def spread(cols, tag):
            bank = ps.tile([P, PACK, P], F32, name=tag, tag=tag)
            for t in range(PACK):
                nc.tensor.transpose(bank[:, t, :], cols[:, t : t + 1].to_broadcast([P, P]), ident[:])
            return bank[:].rearrange("p t n -> p n t")

        def woven_tile(name):
            return sb.tile([P, P * PACK], BF16, name=name + "_woven", tag=name + "_woven", align_bytes=64)

        def before_pick(c, width, dtype):
            return sb.tile([P, width], dtype, name="picked%d" % c, tag="picked%d" % c, align_bytes=64)

        def turn(rows, woven, tag="turn", bufs=3):
            words = rows[:].bitcast(F32)
            bank = ps.tile([P, 2, P], F32, name=tag, tag=tag, bufs=bufs)
            for u in range(2):
                nc.tensor.transpose(bank[:, u, :], words[:, u : I // 2 : 2], ident[:])
            nc.scalar.copy(
                woven.bitcast(F32).rearrange("p (x u) -> p x u", u=2), bank[:].rearrange("p u x -> p x u")
            )
            return woven

        def quantise(woven, codes, name):
            scales = sb.tile([P, P], U8, name=name + "_scales", align_bytes=64)
            nc.vector.quantize_mx(out=codes[:].bitcast(FP8X4), scales=scales[:], in_=woven[:])
            return scales

        def pick(c, woven, **bank):
            picked = before_pick(c, I, BF16)
            nc.vector.tensor_copy(picked[:], val_pools[c][:].indirect(offsets[:]))
            return turn(picked, woven, **bank)

        for quad in range(4):
            live = slice(32 * quad, 32 * quad + 4)
            nc.vector.tensor_copy(scale_pool[live, :].bitcast(I32), scale_rows[live, :].bitcast(I32))
        key_scales = sb.tile([P, I], U8, name="key_scales", align_bytes=64)
        nc.vector.tensor_copy(key_scales[:], scale_pool[:].indirect(offsets[:]))
        q_woven = sb.tile([P, Q * PACK], BF16, name="q_woven", align_bytes=64)
        nc.scalar.copy(q_woven[:].rearrange("p (q t) -> p q t", t=PACK), q_raw[:].rearrange("p t q -> p q t"))
        q_codes = sb.tile([P, Q], U32, name="q_codes", align_bytes=64)
        q_scales = quantise(q_woven, q_codes, "q")
        key_codes = before_pick(0, I, U32)
        nc.vector.tensor_copy(key_codes[:], key_pool[:].indirect(offsets[:]))
        scores = ps.tile([P, I], F32, name="scores", tag="scores")
        nc.tensor.matmul_mx(
            out=scores[:],
            lhsT=q_codes[:].bitcast(FP8X4),
            lhsT_scale=q_scales[:],
            rhs=key_codes[:].bitcast(FP8X4),
            rhs_scale=key_scales[:],
            start=True,
            stop=True,
        )

        size_rows = sb.tile([P, I], F32, name="size_rows")
        nc.scalar.copy(size_rows[:].rearrange("p (n t) -> p n t", t=PACK), spread(size4, "first_turn"))

        neg_max = sb.tile([P, 1], F32, name="neg_max")
        nc.vector.tensor_reduce(neg_max[:], scores[:], mybir.AxisListType.X, ALU.max, negate=True)
        probs = before_pick(2, I, F32)
        row_sum = sb.tile([P, 1], F32, name="row_sum", tag="early_woven", align_bytes=64)
        nc.scalar.activation(probs[:], scores[:], ACT.Exp, bias=neg_max[:], accum_out=row_sum[:])
        inv_sum = sb.tile([P, 1], F32, name="inv_sum")
        nc.scalar.activation(inv_sum[:], row_sum[:], ACT.Abs_reciprocal_sqrt, scale=row_sum[:])

        gain_gate = sb.tile([P, E], F32, name="gain_gate")
        nc.scalar.activation(
            gain_gate[:].rearrange("p (n t) -> p n t", t=PACK), spread(gain4, "scores"), ACT.Copy, scale=gate_col[:]
        )

        early_woven = sb.tile([P, BLOCKS * I], BF16, name="early_woven", tag="early_woven", align_bytes=64)
        pick(0, early_woven[:, 0:I], tag="first_turn", bufs=1)
        pick(1, early_woven[:, I : 2 * I])
        weights = after_pick(1, 0, I, BF16, "weights")
        nc.vector.scalar_tensor_tensor(weights[:], probs[:], inv_sum[:], size_rows[:], ALU.mult, ALU.mult)
        turn(weights, early_woven[:, 3 * I : 4 * I])
        pick(2, early_woven[:, 2 * I : 3 * I], tag="scores", bufs=1)
        last_woven = woven_tile("last")
        pick(3, last_woven[:])

        early_codes = after_pick(3, 1, BLOCKS * P, U32, "early_codes")
        early_scales = sb.tile([P, BLOCKS * P], U8, name="early_scales", align_bytes=64)
        nc.vector.quantize_mx(out=early_codes[:].bitcast(FP8X4), scales=early_scales[:], in_=early_woven[:])
        last_codes = sb.tile([P, P], U32, name="last_codes", align_bytes=64)
        last_scales = quantise(last_woven, last_codes, "last")

        def multiply(read, codes, scales):
            nc.tensor.matmul_mx(
                out=read,
                lhsT=early_codes[:, EARLY:E].bitcast(FP8X4),
                lhsT_scale=early_scales[:, EARLY:E],
                rhs=codes.bitcast(FP8X4),
                rhs_scale=scales,
                start=True,
                stop=True,
            )

        early_read = ps.tile([P, EARLY], F32, name="early_read")
        for cols in (slice(0, HALF), slice(HALF, EARLY)):
            multiply(early_read[:, cols], early_codes[:, cols], early_scales[:, cols])
        last_read = ps.tile([P, P], F32, name="last_read")
        multiply(last_read[:], last_codes[:], last_scales[:])

        squares = sb.tile([P, E], F32, name="squares")
        gained = sb.tile([P, E], F32, name="gained")
        early_sum = sb.tile([P, 1], F32, name="early_sum")
        nc.scalar.activation(squares[:, 0:EARLY], early_read[:], ACT.Square, accum_out=early_sum[:])
        nc.vector.tensor_tensor(gained[:, 0:EARLY], early_read[:], gain_gate[:, 0:EARLY], ALU.mult)
        early_mean = sb.tile([P, 1], F32, name="early_mean")
        nc.scalar.activation(early_mean[:], early_sum[:], ACT.Copy, bias=EPS, scale=1.0 / E)
        last_sum = sb.tile([P, 1], F32, name="last_sum")
        nc.scalar.activation(squares[:, EARLY:E], last_read[:], ACT.Square, accum_out=last_sum[:])
        nc.vector.tensor_tensor(gained[:, EARLY:E], last_read[:], gain_gate[:, EARLY:E], ALU.mult)
        inv_rms = sb.tile([P, 1], F32, name="inv_rms")
        nc.scalar.activation(inv_rms[:], last_sum[:], ACT.Abs_reciprocal_sqrt, bias=early_mean[:], scale=1.0 / E)
        result = sb.tile([P, E], F32, name="result")
        for h, queue in enumerate((nc.sync, nc.scalar)):
            cols = slice(h * HALF, (h + 1) * HALF)
            nc.vector.scalar_tensor_tensor(
                result[:, cols], gained[:, cols], inv_rms[:], res_sb[:, cols], ALU.mult, ALU.add
            )
            queue.dma_start(out[:, cols], result[:, cols])
